import numpy as np
CORES = [0,8,16,24,32,40,48,56,64,72,80,88,96,104,112,120]
N = 16
def setup_inputs(rng):
    return {"x": rng.standard_normal((N, 128, 1024), dtype=np.float32)}
def reference(x):
    s = np.cumsum(x.astype(np.float64), axis=0)
    return {"y": s.astype(x.dtype)}

@@ -1,0 +1,94 @@
+from concourse.bass import DstId, RemoteDMATransfer
+from concourse.mybir import AluOpType
+
+Q = (2, 6, 3, 7)
+NCH = 16
+LAST = 14
+
+SCRATCH = {
+    "xs": ("dram", [64, 128, 16], "float32"),
+    "rb": ("dram", [16, 128, 16], "float32"),
+    "gb": ("dram", [16, 128, 16], "float32"),
+    "land": ("dram", [64, 128, 16], "float32"),
+}
+SEMAPHORES = ["ld0", "ld1", "ld2", "ld3", "h0", "h1", "sent",
+              "land0", "land1", "land2", "land3", "cp", "st", "acc"]
+
+
+def _dst(topo, core):
+    rid, pid, _se = topo.addr(core)
+    return DstId(rid=rid, pnc=pid)
+
+
+def _rank_core(g, r, T, topo):
+    queues = (g.sync, g.scalar)
+    if r <= LAST:
+        for qi in range(4):
+            queues[qi % 2].dma_start(T.xs[16 * qi:16 * qi + 16], T.x[32 * qi:32 * qi + 32, :]).then_inc(
+                T.sem["ld%d" % qi], 16)
+        for qi in range(4):
+            g.wait_ge(T.sem["ld%d" % qi], 16)
+            d = _dst(topo, 8 * r + Q[qi])
+            g.remote_dma_fused(
+                [RemoteDMATransfer(dst_ids=[d], dma_engine_mask=1 << c, remote_sem=T.sem.h0,
+                                   src=T.xs[16 * qi + c], dst=T.rb[c], alu_op=0) for c in range(NCH)],
+                local_sem=T.sem.sent)
+    if r % 2 == 1 or r == 0:
+        if r <= LAST:
+            g.sync.wait_ge(T.sem.sent, 64)
+        g.sync.dma_start(T.y[:], T.x[:]).then_inc(T.sem.cp, 16)
+        g.wait_ge(T.sem.cp, 16)
+    if r % 2 == 1:
+        for qi in range(4):
+            g.wait_ge(T.sem["land%d" % qi], 32)
+            g.dma_start(T.y[32 * qi:32 * qi + 32, :], T.land[16 * qi:16 * qi + 16], accum_op=AluOpType.add,
+                        max_dma_last_dim=8192).then_inc(T.sem.acc, 16)
+        g.wait_ge(T.sem.acc, 64)
+    elif r > 0:
+        for qi in range(4):
+            qq = queues[qi % 2]
+            qq.wait_ge(T.sem["land%d" % qi], 32)
+            qq.dma_start(T.y[32 * qi:32 * qi + 32, :], T.land[16 * qi:16 * qi + 16]).then_inc(T.sem.st, 16)
+        g.wait_ge(T.sem.st, 64)
+    if r <= LAST:
+        g.wait_ge(T.sem.sent, 64)
+
+
+def _owner_core(g, c, qi, T, topo):
+    q = Q[qi]
+    sent = 0
+    if c <= LAST:
+        g.wait_ge(T.sem.h0, 16)
+        others = [(c + k) % NCH for k in range(1, NCH)]
+        for part in (others[:8], others[8:]):
+            g.remote_dma_fused(
+                [RemoteDMATransfer(dst_ids=[_dst(topo, 8 * c2 + q)], dma_engine_mask=1 << e, remote_sem=T.sem.h1,
+                                   src=T.rb[c2], dst=T.gb[c], alu_op=0) for e, c2 in enumerate(part)],
+                local_sem=T.sem.sent)
+            sent += len(part)
+    g.wait_ge(T.sem.h1, LAST if c <= LAST else LAST + 1)
+
+    def src(i):
+        return T.rb[c] if i == c else T.gb[i]
+
+    u = 16 * qi + c
+    for ms in ((7, 6, 5, 4), (0, 1, 2, 3)):
+        trs = []
+        for j, m in enumerate(ms):
+            ranks = ([2 * m] if m else []) + [2 * m + 1]
+            srcs = [src(i) for i in range(2 * m + 1)]
+            trs.append(RemoteDMATransfer(
+                dst_ids=[_dst(topo, 8 * rr) for rr in ranks], dma_engine_mask=3 << (2 * j),
+                remote_sem=T.sem["land%d" % qi], srcs=srcs, dsts=[T.land[u] for _rr in ranks],
+                alu_op=1 if len(srcs) > 1 else 0))
+            sent += 2
+        g.remote_dma_fused(trs, local_sem=T.sem.sent)
+    g.wait_ge(T.sem.sent, sent)
+
+
+def rank_program(g, core, T, topo):
+    c, k = divmod(core, 8)
+    if k == 0:
+        _rank_core(g, c, T, topo)
+    elif k in Q:
+        _owner_core(g, c, Q.index(k), T, topo)

@@ -4,6 +4,8 @@ from concourse.mybir import AluOpType
 Q = (2, 6, 3, 7)
 NCH = 16
 LAST = 14
+SPLIT = 8
+CSLOT = 15
 
 SCRATCH = {
     "xs": ("dram", [64, 128, 16], "float32"),
@@ -11,13 +13,17 @@ SCRATCH = {
     "gb": ("dram", [16, 128, 16], "float32"),
     "land": ("dram", [64, 128, 16], "float32"),
 }
-SEMAPHORES = ["ld0", "ld1", "ld2", "ld3", "h0", "h1", "sent",
+SEMAPHORES = ["ld0", "ld1", "ld2", "ld3", "h0", "lo", "up", "cs", "sent",
               "land0", "land1", "land2", "land3", "cp", "st", "acc"]
 
 
 def _dst(topo, core):
     rid, pid, _se = topo.addr(core)
     return DstId(rid=rid, pnc=pid)
+
+
+def _home(c, qi):
+    return (Q[qi], "lo") if c < SPLIT else (Q[qi ^ 1], "up")
 
 
 def _rank_core(g, r, T, topo):
@@ -28,11 +34,16 @@ def _rank_core(g, r, T, topo):
                 T.sem["ld%d" % qi], 16)
         for qi in range(4):
             g.wait_ge(T.sem["ld%d" % qi], 16)
-            d = _dst(topo, 8 * r + Q[qi])
-            g.remote_dma_fused(
-                [RemoteDMATransfer(dst_ids=[d], dma_engine_mask=1 << c, remote_sem=T.sem.h0,
-                                   src=T.xs[16 * qi + c], dst=T.rb[c], alu_op=0) for c in range(NCH)],
-                local_sem=T.sem.sent)
+            hk, hs = _home(r, qi)
+            trs = []
+            for c in range(NCH):
+                if c == r:
+                    trs.append(RemoteDMATransfer(dst_ids=[_dst(topo, 8 * r + hk)], dma_engine_mask=1 << c,
+                                                 remote_sem=T.sem[hs], src=T.xs[16 * qi + c], dst=T.gb[r], alu_op=0))
+                else:
+                    trs.append(RemoteDMATransfer(dst_ids=[_dst(topo, 8 * r + Q[qi])], dma_engine_mask=1 << c,
+                                                 remote_sem=T.sem.h0, src=T.xs[16 * qi + c], dst=T.rb[c], alu_op=0))
+            g.remote_dma_fused(trs, local_sem=T.sem.sent)
     if r % 2 == 1 or r == 0:
         if r <= LAST:
             g.sync.wait_ge(T.sem.sent, 64)
@@ -54,35 +65,42 @@ def _rank_core(g, r, T, topo):
         g.wait_ge(T.sem.sent, 64)
 
 
+def _prefix_call(g, T, topo, quarter, c, jobs):
+    trs = []
+    for j, (m, srcs) in enumerate(jobs):
+        ranks = ([2 * m] if m else []) + [2 * m + 1]
+        trs.append(RemoteDMATransfer(
+            dst_ids=[_dst(topo, 8 * rr) for rr in ranks], dma_engine_mask=3 << (2 * j),
+            remote_sem=T.sem["land%d" % quarter], srcs=srcs, dsts=[T.land[16 * quarter + c] for _rr in ranks],
+            alu_op=1 if len(srcs) > 1 else 0))
+    g.remote_dma_fused(trs, local_sem=T.sem.sent)
+    return 2 * len(jobs)
+
+
 def _owner_core(g, c, qi, T, topo):
-    q = Q[qi]
+    pi = qi ^ 1
     sent = 0
     if c <= LAST:
-        g.wait_ge(T.sem.h0, 16)
+        g.wait_ge(T.sem.h0, 15)
+        hk, hs = _home(c, qi)
         others = [(c + k) % NCH for k in range(1, NCH)]
         for part in (others[:8], others[8:]):
             g.remote_dma_fused(
-                [RemoteDMATransfer(dst_ids=[_dst(topo, 8 * c2 + q)], dma_engine_mask=1 << e, remote_sem=T.sem.h1,
+                [RemoteDMATransfer(dst_ids=[_dst(topo, 8 * c2 + hk)], dma_engine_mask=1 << e, remote_sem=T.sem[hs],
                                    src=T.rb[c2], dst=T.gb[c], alu_op=0) for e, c2 in enumerate(part)],
                 local_sem=T.sem.sent)
             sent += len(part)
-    g.wait_ge(T.sem.h1, LAST if c <= LAST else LAST + 1)
-
-    def src(i):
-        return T.rb[c] if i == c else T.gb[i]
-
-    u = 16 * qi + c
-    for ms in ((7, 6, 5, 4), (0, 1, 2, 3)):
-        trs = []
-        for j, m in enumerate(ms):
-            ranks = ([2 * m] if m else []) + [2 * m + 1]
-            srcs = [src(i) for i in range(2 * m + 1)]
-            trs.append(RemoteDMATransfer(
-                dst_ids=[_dst(topo, 8 * rr) for rr in ranks], dma_engine_mask=3 << (2 * j),
-                remote_sem=T.sem["land%d" % qi], srcs=srcs, dsts=[T.land[u] for _rr in ranks],
-                alu_op=1 if len(srcs) > 1 else 0))
-            sent += 2
-        g.remote_dma_fused(trs, local_sem=T.sem.sent)
+    g.wait_ge(T.sem.lo, SPLIT)
+    g.remote_dma_fused(
+        [RemoteDMATransfer(dst_ids=[_dst(topo, 8 * c + Q[pi])], dma_engine_mask=0xFF00, remote_sem=T.sem.cs,
+                           srcs=[T.gb[i] for i in range(SPLIT)], dsts=[T.gb[CSLOT]], alu_op=1)],
+        local_sem=T.sem.sent)
+    sent += 8
+    sent += _prefix_call(g, T, topo, qi, c, [(m, [T.gb[i] for i in range(2 * m + 1)]) for m in (3, 2, 1, 0)])
+    g.wait_ge(T.sem.up, LAST + 1 - SPLIT)
+    g.wait_ge(T.sem.cs, 8)
+    sent += _prefix_call(g, T, topo, pi, c,
+                         [(m, [T.gb[CSLOT]] + [T.gb[i] for i in range(SPLIT, 2 * m + 1)]) for m in (4, 5, 6, 7)])
     g.wait_ge(T.sem.sent, sent)
 
 

@@ -2,6 +2,7 @@ from concourse.bass import DstId, RemoteDMATransfer
 from concourse.mybir import AluOpType
 
 Q = (2, 6, 3, 7)
+HELP = (1, 4, 0, 5)
 NCH = 16
 LAST = 14
 SPLIT = 8
@@ -26,6 +27,19 @@ def _home(c, qi):
     return (Q[qi], "lo") if c < SPLIT else (Q[qi ^ 1], "up")
 
 
+def _same(c):
+    return [c2 for c2 in range(NCH) if c2 != c and (c2 - c) % 2 == 0]
+
+
+def _cross(c):
+    return [c2 for c2 in range(NCH) if (c2 - c) % 2 == 1]
+
+
+def _copy(T, topo, core, engine, sem, src, dst):
+    return RemoteDMATransfer(dst_ids=[_dst(topo, core)], dma_engine_mask=1 << engine, remote_sem=T.sem[sem],
+                             src=src, dst=dst, alu_op=0)
+
+
 def _rank_core(g, r, T, topo):
     queues = (g.sync, g.scalar)
     if r <= LAST:
@@ -36,13 +50,14 @@ def _rank_core(g, r, T, topo):
             g.wait_ge(T.sem["ld%d" % qi], 16)
             hk, hs = _home(r, qi)
             trs = []
-            for c in range(NCH):
-                if c == r:
-                    trs.append(RemoteDMATransfer(dst_ids=[_dst(topo, 8 * r + hk)], dma_engine_mask=1 << c,
-                                                 remote_sem=T.sem[hs], src=T.xs[16 * qi + c], dst=T.gb[r], alu_op=0))
+            for c in _same(r):
+                if HELP[qi] == 0:
+                    trs.append(_copy(T, topo, 8 * c + hk, len(trs), hs, T.xs[16 * qi + c], T.gb[r]))
                 else:
-                    trs.append(RemoteDMATransfer(dst_ids=[_dst(topo, 8 * r + Q[qi])], dma_engine_mask=1 << c,
-                                                 remote_sem=T.sem.h0, src=T.xs[16 * qi + c], dst=T.rb[c], alu_op=0))
+                    trs.append(_copy(T, topo, 8 * r + HELP[qi], len(trs), "h0", T.xs[16 * qi + c], T.rb[c]))
+            for c in _cross(r):
+                trs.append(_copy(T, topo, 8 * r + Q[qi], len(trs), "h0", T.xs[16 * qi + c], T.rb[c]))
+            trs.append(_copy(T, topo, 8 * r + hk, len(trs), hs, T.xs[16 * qi + r], T.gb[r]))
             g.remote_dma_fused(trs, local_sem=T.sem.sent)
     if r % 2 == 1 or r == 0:
         if r <= LAST:
@@ -65,6 +80,14 @@ def _rank_core(g, r, T, topo):
         g.wait_ge(T.sem.sent, 64)
 
 
+def _pass_on(g, c, qi, chips, T, topo):
+    g.wait_ge(T.sem.h0, len(chips))
+    hk, hs = _home(c, qi)
+    g.remote_dma_fused([_copy(T, topo, 8 * c2 + hk, e, hs, T.rb[c2], T.gb[c]) for e, c2 in enumerate(chips)],
+                       local_sem=T.sem.sent)
+    return len(chips)
+
+
 def _prefix_call(g, T, topo, quarter, c, jobs):
     trs = []
     for j, (m, srcs) in enumerate(jobs):
@@ -81,15 +104,7 @@ def _owner_core(g, c, qi, T, topo):
     pi = qi ^ 1
     sent = 0
     if c <= LAST:
-        g.wait_ge(T.sem.h0, 15)
-        hk, hs = _home(c, qi)
-        others = [(c + k) % NCH for k in range(1, NCH)]
-        for part in (others[:8], others[8:]):
-            g.remote_dma_fused(
-                [RemoteDMATransfer(dst_ids=[_dst(topo, 8 * c2 + hk)], dma_engine_mask=1 << e, remote_sem=T.sem[hs],
-                                   src=T.rb[c2], dst=T.gb[c], alu_op=0) for e, c2 in enumerate(part)],
-                local_sem=T.sem.sent)
-            sent += len(part)
+        sent += _pass_on(g, c, qi, _cross(c), T, topo)
     g.wait_ge(T.sem.lo, SPLIT)
     g.remote_dma_fused(
         [RemoteDMATransfer(dst_ids=[_dst(topo, 8 * c + Q[pi])], dma_engine_mask=0xFF00, remote_sem=T.sem.cs,
@@ -110,3 +125,5 @@ def rank_program(g, core, T, topo):
         _rank_core(g, c, T, topo)
     elif k in Q:
         _owner_core(g, c, Q.index(k), T, topo)
+    elif c <= LAST:
+        g.wait_ge(T.sem.sent, _pass_on(g, c, HELP.index(k), _same(c), T, topo))

@@ -14,7 +14,7 @@ SCRATCH = {
     "gb": ("dram", [16, 128, 16], "float32"),
     "land": ("dram", [64, 128, 16], "float32"),
 }
-SEMAPHORES = ["ld0", "ld1", "ld2", "ld3", "h0", "lo", "up", "cs", "sent",
+SEMAPHORES = ["ld0", "ld1", "ld2", "ld3", "h0", "lo", "up", "cs", "us", "sent", "sentu",
               "land0", "land1", "land2", "land3", "cp", "st", "acc"]
 
 
@@ -24,7 +24,7 @@ def _dst(topo, core):
 
 
 def _home(c, qi):
-    return (Q[qi], "lo") if c < SPLIT else (Q[qi ^ 1], "up")
+    return (Q[qi], "lo") if c < SPLIT else (HELP[qi], "up")
 
 
 def _same(c):
@@ -40,8 +40,21 @@ def _copy(T, topo, core, engine, sem, src, dst):
                              src=src, dst=dst, alu_op=0)
 
 
+def _upper_sums(g, c, qi, T, topo):
+    mine = HELP[qi] == 0 and SPLIT <= c <= LAST
+    g.wait_ge(T.sem.up, LAST + 1 - SPLIT - (1 if mine else 0))
+    trs = []
+    for j, m in enumerate((4, 5, 6, 7)):
+        srcs = [T.xs[16 * qi + c] if (mine and i == c) else T.gb[i] for i in range(SPLIT, 2 * m + 1)]
+        trs.append(RemoteDMATransfer(dst_ids=[_dst(topo, 8 * c + Q[qi ^ 1])], dma_engine_mask=15 << (4 * j),
+                                     remote_sem=T.sem.us, srcs=srcs, dsts=[T.gb[SPLIT + j]],
+                                     alu_op=1 if len(srcs) > 1 else 0))
+    g.remote_dma_fused(trs, local_sem=T.sem.sentu)
+
+
 def _rank_core(g, r, T, topo):
     queues = (g.sync, g.scalar)
+    sent = 0
     if r <= LAST:
         for qi in range(4):
             queues[qi % 2].dma_start(T.xs[16 * qi:16 * qi + 16], T.x[32 * qi:32 * qi + 32, :]).then_inc(
@@ -57,12 +70,16 @@ def _rank_core(g, r, T, topo):
                     trs.append(_copy(T, topo, 8 * r + HELP[qi], len(trs), "h0", T.xs[16 * qi + c], T.rb[c]))
             for c in _cross(r):
                 trs.append(_copy(T, topo, 8 * r + Q[qi], len(trs), "h0", T.xs[16 * qi + c], T.rb[c]))
-            trs.append(_copy(T, topo, 8 * r + hk, len(trs), hs, T.xs[16 * qi + r], T.gb[r]))
+            if hk != 0:
+                trs.append(_copy(T, topo, 8 * r + hk, len(trs), hs, T.xs[16 * qi + r], T.gb[r]))
             g.remote_dma_fused(trs, local_sem=T.sem.sent)
+            sent += len(trs)
     if r % 2 == 1 or r == 0:
         if r <= LAST:
-            g.sync.wait_ge(T.sem.sent, 64)
+            g.sync.wait_ge(T.sem.sent, sent)
         g.sync.dma_start(T.y[:], T.x[:]).then_inc(T.sem.cp, 16)
+    _upper_sums(g, r, HELP.index(0), T, topo)
+    if r % 2 == 1 or r == 0:
         g.wait_ge(T.sem.cp, 16)
     if r % 2 == 1:
         for qi in range(4):
@@ -77,7 +94,8 @@ def _rank_core(g, r, T, topo):
             qq.dma_start(T.y[32 * qi:32 * qi + 32, :], T.land[16 * qi:16 * qi + 16]).then_inc(T.sem.st, 16)
         g.wait_ge(T.sem.st, 64)
     if r <= LAST:
-        g.wait_ge(T.sem.sent, 64)
+        g.wait_ge(T.sem.sent, sent)
+    g.wait_ge(T.sem.sentu, 16)
 
 
 def _pass_on(g, c, qi, chips, T, topo):
@@ -112,10 +130,9 @@ def _owner_core(g, c, qi, T, topo):
         local_sem=T.sem.sent)
     sent += 8
     sent += _prefix_call(g, T, topo, qi, c, [(m, [T.gb[i] for i in range(2 * m + 1)]) for m in (3, 2, 1, 0)])
-    g.wait_ge(T.sem.up, LAST + 1 - SPLIT)
     g.wait_ge(T.sem.cs, 8)
-    sent += _prefix_call(g, T, topo, pi, c,
-                         [(m, [T.gb[CSLOT]] + [T.gb[i] for i in range(SPLIT, 2 * m + 1)]) for m in (4, 5, 6, 7)])
+    g.wait_ge(T.sem.us, 16)
+    sent += _prefix_call(g, T, topo, pi, c, [(m, [T.gb[CSLOT], T.gb[SPLIT + m - 4]]) for m in (4, 5, 6, 7)])
     g.wait_ge(T.sem.sent, sent)
 
 
@@ -125,5 +142,10 @@ def rank_program(g, core, T, topo):
         _rank_core(g, c, T, topo)
     elif k in Q:
         _owner_core(g, c, Q.index(k), T, topo)
-    elif c <= LAST:
-        g.wait_ge(T.sem.sent, _pass_on(g, c, HELP.index(k), _same(c), T, topo))
+    else:
+        qi = HELP.index(k)
+        n = _pass_on(g, c, qi, _same(c), T, topo) if c <= LAST else 0
+        _upper_sums(g, c, qi, T, topo)
+        if n:
+            g.wait_ge(T.sem.sent, n)
+        g.wait_ge(T.sem.sentu, 16)

from concourse.bass import DstId, RemoteDMATransfer
from concourse.mybir import AluOpType

Q = (2, 6, 3, 7)
HELP = (1, 4, 0, 5)
NCH = 16
LAST = 14
SPLIT = 8
CSLOT = 15

SCRATCH = {
    "xs": ("dram", [64, 128, 16], "float32"),
    "rb": ("dram", [16, 128, 16], "float32"),
    "gb": ("dram", [16, 128, 16], "float32"),
    "land": ("dram", [64, 128, 16], "float32"),
}
SEMAPHORES = ["ld0", "ld1", "ld2", "ld3", "h0", "lo", "up", "cs", "us", "sent", "sentu",
              "land0", "land1", "land2", "land3", "cp", "st", "acc"]


def _dst(topo, core):
    rid, pid, _se = topo.addr(core)
    return DstId(rid=rid, pnc=pid)


def _home(c, qi):
    return (Q[qi], "lo") if c < SPLIT else (HELP[qi], "up")


def _same(c):
    return [c2 for c2 in range(NCH) if c2 != c and (c2 - c) % 2 == 0]


def _cross(c):
    return [c2 for c2 in range(NCH) if (c2 - c) % 2 == 1]


def _copy(T, topo, core, engine, sem, src, dst):
    return RemoteDMATransfer(dst_ids=[_dst(topo, core)], dma_engine_mask=1 << engine, remote_sem=T.sem[sem],
                             src=src, dst=dst, alu_op=0)


def _upper_sums(g, c, qi, T, topo):
    mine = HELP[qi] == 0 and SPLIT <= c <= LAST
    g.wait_ge(T.sem.up, LAST + 1 - SPLIT - (1 if mine else 0))
    trs = []
    for j, m in enumerate((4, 5, 6, 7)):
        srcs = [T.xs[16 * qi + c] if (mine and i == c) else T.gb[i] for i in range(SPLIT, 2 * m + 1)]
        trs.append(RemoteDMATransfer(dst_ids=[_dst(topo, 8 * c + Q[qi ^ 1])], dma_engine_mask=15 << (4 * j),
                                     remote_sem=T.sem.us, srcs=srcs, dsts=[T.gb[SPLIT + j]],
                                     alu_op=1 if len(srcs) > 1 else 0))
    g.remote_dma_fused(trs, local_sem=T.sem.sentu)


def _rank_core(g, r, T, topo):
    queues = (g.sync, g.scalar)
    sent = 0
    if r <= LAST:
        for qi in range(4):
            queues[qi % 2].dma_start(T.xs[16 * qi:16 * qi + 16], T.x[32 * qi:32 * qi + 32, :]).then_inc(
                T.sem["ld%d" % qi], 16)
        for qi in range(4):
            g.wait_ge(T.sem["ld%d" % qi], 16)
            hk, hs = _home(r, qi)
            trs = []
            for c in _same(r):
                if HELP[qi] == 0:
                    trs.append(_copy(T, topo, 8 * c + hk, len(trs), hs, T.xs[16 * qi + c], T.gb[r]))
                else:
                    trs.append(_copy(T, topo, 8 * r + HELP[qi], len(trs), "h0", T.xs[16 * qi + c], T.rb[c]))
            for c in _cross(r):
                trs.append(_copy(T, topo, 8 * r + Q[qi], len(trs), "h0", T.xs[16 * qi + c], T.rb[c]))
            if hk != 0:
                trs.append(_copy(T, topo, 8 * r + hk, len(trs), hs, T.xs[16 * qi + r], T.gb[r]))
            g.remote_dma_fused(trs, local_sem=T.sem.sent)
            sent += len(trs)
    if r % 2 == 1 or r == 0:
        if r <= LAST:
            g.sync.wait_ge(T.sem.sent, sent)
        g.sync.dma_start(T.y[:], T.x[:]).then_inc(T.sem.cp, 16)
    _upper_sums(g, r, HELP.index(0), T, topo)
    if r % 2 == 1 or r == 0:
        g.wait_ge(T.sem.cp, 16)
    if r % 2 == 1:
        for qi in range(4):
            g.wait_ge(T.sem["land%d" % qi], 32)
            g.dma_start(T.y[32 * qi:32 * qi + 32, :], T.land[16 * qi:16 * qi + 16], accum_op=AluOpType.add,
                        max_dma_last_dim=8192).then_inc(T.sem.acc, 16)
        g.wait_ge(T.sem.acc, 64)
    elif r > 0:
        for qi in range(4):
            qq = queues[qi % 2]
            qq.wait_ge(T.sem["land%d" % qi], 32)
            qq.dma_start(T.y[32 * qi:32 * qi + 32, :], T.land[16 * qi:16 * qi + 16]).then_inc(T.sem.st, 16)
        g.wait_ge(T.sem.st, 64)
    if r <= LAST:
        g.wait_ge(T.sem.sent, sent)
    g.wait_ge(T.sem.sentu, 16)


def _pass_on(g, c, qi, chips, T, topo):
    g.wait_ge(T.sem.h0, len(chips))
    hk, hs = _home(c, qi)
    g.remote_dma_fused([_copy(T, topo, 8 * c2 + hk, e, hs, T.rb[c2], T.gb[c]) for e, c2 in enumerate(chips)],
                       local_sem=T.sem.sent)
    return len(chips)


def _prefix_call(g, T, topo, quarter, c, jobs):
    trs = []
    for j, (m, srcs) in enumerate(jobs):
        ranks = ([2 * m] if m else []) + [2 * m + 1]
        trs.append(RemoteDMATransfer(
            dst_ids=[_dst(topo, 8 * rr) for rr in ranks], dma_engine_mask=3 << (2 * j),
            remote_sem=T.sem["land%d" % quarter], srcs=srcs, dsts=[T.land[16 * quarter + c] for _rr in ranks],
            alu_op=1 if len(srcs) > 1 else 0))
    g.remote_dma_fused(trs, local_sem=T.sem.sent)
    return 2 * len(jobs)


def _owner_core(g, c, qi, T, topo):
    pi = qi ^ 1
    sent = 0
    if c <= LAST:
        sent += _pass_on(g, c, qi, _cross(c), T, topo)
    g.wait_ge(T.sem.lo, SPLIT)
    g.remote_dma_fused(
        [RemoteDMATransfer(dst_ids=[_dst(topo, 8 * c + Q[pi])], dma_engine_mask=0xFF00, remote_sem=T.sem.cs,
                           srcs=[T.gb[i] for i in range(SPLIT)], dsts=[T.gb[CSLOT]], alu_op=1)],
        local_sem=T.sem.sent)
    sent += 8
    sent += _prefix_call(g, T, topo, qi, c, [(m, [T.gb[i] for i in range(2 * m + 1)]) for m in (3, 2, 1, 0)])
    g.wait_ge(T.sem.cs, 8)
    g.wait_ge(T.sem.us, 16)
    sent += _prefix_call(g, T, topo, pi, c, [(m, [T.gb[CSLOT], T.gb[SPLIT + m - 4]]) for m in (4, 5, 6, 7)])
    g.wait_ge(T.sem.sent, sent)


def rank_program(g, core, T, topo):
    c, k = divmod(core, 8)
    if k == 0:
        _rank_core(g, c, T, topo)
    elif k in Q:
        _owner_core(g, c, Q.index(k), T, topo)
    else:
        qi = HELP.index(k)
        n = _pass_on(g, c, qi, _same(c), T, topo) if c <= LAST else 0
        _upper_sums(g, c, qi, T, topo)
        if n:
            g.wait_ge(T.sem.sent, n)
        g.wait_ge(T.sem.sentu, 16)
